import numpy as np, ml_dtypes
CORES = [24,25,26,27,48,49,50,51,72,73,74,75,96,97,98,99]
N = 16
KB, QP = 1, 256
MEM = [7,10]
WID = [192,256,32,160,96,256,160,256,32,192,256,160,192,64,192,64]
def setup_inputs(rng):
    return {"q": rng.standard_normal((N, 128, QP), dtype=np.float32).astype(ml_dtypes.bfloat16), "k": rng.standard_normal((N, 128, KB * 128), dtype=np.float32).astype(ml_dtypes.bfloat16), "v": rng.standard_normal((N, 128, KB * 128), dtype=np.float32).astype(ml_dtypes.bfloat16)}
def setup_inputs_big(rng):
    d = setup_inputs(rng)
    for k in ("q", "k", "v"): d[k] = (d[k].astype(np.float32) * 1024.0).astype(d[k].dtype)
    return d
def setup_inputs_small(rng):
    d = setup_inputs(rng)
    for k in ("q", "k", "v"): d[k] = (d[k].astype(np.float32) * (1 / 1024.0)).astype(d[k].dtype)
    return d
def setup_inputs_apart(rng):
    d = setup_inputs(rng)
    f = (10.0 ** rng.permutation(np.linspace(-1.5, 1.5, N))).astype(np.float32).reshape(N, 1, 1)
    for k in ("q", "k", "v"): d[k] = (d[k].astype(np.float32) * f).astype(d[k].dtype)
    return d
def whole(q, k, v):
    Q, K, V = q.astype(np.float64), k.astype(np.float64), v.astype(np.float64)
    y = np.zeros((N, 128, QP))
    for r in range(N):
        for j in MEM:
            for b in range(KB):
                S = np.maximum(K[j][:, 128 * b:128 * b + 128].T @ Q[r], 0.0)
                y[r] += V[j][:, 128 * b:128 * b + 128].T @ S
    return {"y": y.astype(ml_dtypes.bfloat16 if q.dtype != np.float64 else np.float64)}
def reference(q, k, v):
    o = whole(q, k, v)["y"].copy()
    for r in range(N):
        o[r][:, WID[r]:] = np.nan
    return {"y": o}

@@ -1,0 +1,191 @@
+from concourse.bass import DstId, RemoteDMATransfer
+from concourse.mybir import AluOpType
+
+QP = 256
+KP = 128
+NB = 4
+
+SCRATCH = {
+    "kv": ("sbuf", [128, 2 * KP], "bfloat16"),
+    "qall": ("sbuf", [128, NB * QP], "bfloat16"),
+    "zero": ("sbuf", [128, QP], "float32"),
+    "srel": ("sbuf", [128, NB * QP], "bfloat16"),
+    "obuf": ("sbuf", [128, NB * QP], "bfloat16"),
+    "land": ("sbuf", [128, 2 * QP], "bfloat16"),
+    "ybuf": ("sbuf", [128, QP], "bfloat16"),
+}
+for _b in range(NB):
+    SCRATCH["ps%d" % _b] = ("psum", [128, 512], "float32")
+    SCRATCH["po%d" % _b] = ("psum", [128, 512], "float32")
+
+SEMAPHORES = ["ldkv", "ldq", "kva", "pa0", "pa1", "zs", "fin", "st", "snt"]
+for _b in range(NB):
+    SEMAPHORES += ["qa%d" % _b, "sm%d" % _b, "rl%d" % _b, "om%d" % _b, "cp%d" % _b]
+
+
+def _count(m):
+    return bin(m).count("1")
+
+
+def _low(m, n):
+    out, i = 0, 0
+    while n > 0:
+        if (m >> i) & 1:
+            out |= 1 << i
+            n -= 1
+        i += 1
+    return out
+
+
+def _plan(T, topo):
+    cores, wid, mem = T.cores, T.tables["WID"], T.tables["MEM"]
+    chips, members = [], {}
+    for r, c in enumerate(cores):
+        ch = topo.chip(c)
+        if ch not in members:
+            members[ch] = []
+            chips.append(ch)
+        members[ch].append(r)
+    home = [topo.chip(cores[m]) for m in mem]
+    plain = [ch for ch in chips if ch not in home]
+    order = []
+    for ji in range(len(mem)):
+        first = [ch for ch in chips if ch in home and ch != home[ji]]
+        k = ji % len(plain) if plain else 0
+        order.append(first + plain[k:] + plain[:k])
+    hub = {}
+    for ch in chips:
+        h = [mem[ji] if home[ji] == ch else None for ji in range(len(mem))]
+        free = sorted([r for r in members[ch] if r not in mem], key=lambda r: -wid[r])
+        todo = sorted([ji for ji in range(len(mem)) if h[ji] is None], key=lambda ji: -order[ji].index(ch))
+        for ji, r in zip(todo, free):
+            h[ji] = r
+        hub[ch] = h
+
+    def both(src, dsts):
+        m = topo.mask(src, dsts[0])
+        for d in dsts:
+            assert topo.may_write(src, d)
+            m &= topo.mask(src, d)
+        return m
+
+    def kv_dsts(ji):
+        return [cores[hub[ch][ji]] for ch in order[ji]]
+
+    def kv_mask(ji):
+        return both(cores[mem[ji]], kv_dsts(ji))
+
+    def q_dsts(r):
+        return [cores[h] for h in hub[topo.chip(cores[r])] if h != r]
+
+    def q_mask(r):
+        full = both(cores[r], q_dsts(r))
+        if r in mem:
+            return full & ~kv_mask(mem.index(r))
+        if r in hub[topo.chip(cores[r])]:
+            return full
+        return _low(full, _count(full) // 2)
+
+    return members, hub, kv_dsts, kv_mask, q_dsts, q_mask, both
+
+
+def rank_program(g, core, T, topo):
+    rank = T.rank_of(core)
+    if rank is None:
+        return
+    cores, wid, mem = T.cores, T.tables["WID"], T.tables["MEM"]
+    members, hub, kv_dsts, kv_mask, q_dsts, q_mask, both = _plan(T, topo)
+    sem = T.sem
+    mine = members[topo.chip(core)]
+    hubs = hub[topo.chip(core)]
+    slot, W = mine.index(rank), wid[rank]
+    is_mem = rank in mem
+    myj = hubs.index(rank) if rank in hubs else None
+
+    def cols(t, s, w):
+        return t[:, s * QP:s * QP + w]
+
+    def ids(dsts):
+        return [DstId(rid=topo.addr(d)[0], pnc=topo.addr(d)[1]) for d in dsts]
+
+    if is_mem:
+        g.sync.dma_start(T.kv[:, 0:KP], T.k[:, :]).then_inc(sem.ldkv, 16)
+        g.scalar.dma_start(T.kv[:, KP:2 * KP], T.v[:, :]).then_inc(sem.ldkv, 16)
+    g.sync.dma_start(cols(T.qall, slot, W), T.q[:, 0:W]).then_inc(sem.ldq, 16)
+
+    sent = 0
+    if is_mem:
+        ji = mem.index(rank)
+        d = kv_dsts(ji)
+        g.wait_ge(sem.ldkv, 32)
+        g.remote_dma_fused([RemoteDMATransfer(dst_ids=ids(d), dma_engine_mask=kv_mask(ji), remote_sem=sem.kva,
+                                              srcs=[T.kv[:, :]], dsts=[T.kv[:, :] for _ in d])], local_sem=sem.snt)
+        sent += _count(kv_mask(ji))
+    d = q_dsts(rank)
+    g.wait_ge(sem.ldq, 16)
+    g.remote_dma_fused([RemoteDMATransfer(dst_ids=ids(d), dma_engine_mask=q_mask(rank), remote_sem=sem["qa%d" % slot],
+                                          srcs=[cols(T.qall, slot, W)], dsts=[cols(T.qall, slot, W) for _ in d])],
+                       local_sem=sem.snt)
+    sent += _count(q_mask(rank))
+
+    te, ve = g.tensor, g.vector
+    if myj is None:
+        for ji in range(len(mem)):
+            ve.wait_ge(sem["pa%d" % ji], _count(both(cores[hubs[ji]], [core])))
+        ve.tensor_tensor(T.ybuf[:, 0:W], cols(T.land, 0, W), cols(T.land, 1, W), AluOpType.add).then_inc(sem.fin, 1)
+    else:
+        away = sorted([s for s in range(len(mine)) if s != slot], key=lambda s: -wid[mine[s]])
+        bw = {s: wid[mine[s]] for s in range(len(mine))}
+
+        def mm_s(s):
+            if s == slot:
+                te.wait_ge(sem.ldq, 16)
+            else:
+                te.wait_ge(sem["qa%d" % s], _count(q_mask(mine[s])))
+            te.matmul(T["ps%d" % s][:, 0:bw[s]], T.kv[:, 0:KP], cols(T.qall, s, bw[s]), True, True) \
+                .then_inc(sem["sm%d" % s], 1)
+
+        def mm_o(s):
+            te.wait_ge(sem["rl%d" % s], 1)
+            te.matmul(T["po%d" % s][:, 0:bw[s]], T.kv[:, KP:2 * KP], cols(T.srel, s, bw[s]), True, True) \
+                .then_inc(sem["om%d" % s], 1)
+
+        def relu(s):
+            ve.wait_ge(sem["sm%d" % s], 1)
+            ve.tensor_tensor(cols(T.srel, s, bw[s]), T["ps%d" % s][:, 0:bw[s]], T.zero[:, 0:bw[s]], AluOpType.max) \
+                .then_inc(sem["rl%d" % s], 1)
+
+        def out(s):
+            ve.wait_ge(sem["om%d" % s], 1)
+            ve.tensor_copy(cols(T.obuf, s, bw[s]), T["po%d" % s][:, 0:bw[s]]).then_inc(sem["cp%d" % s], 1)
+
+        if is_mem:
+            te.wait_ge(sem.ldkv, 32)
+        else:
+            te.wait_ge(sem.kva, _count(kv_mask(myj)))
+        a, b, c = away
+        for f, s in ((mm_s, a), (mm_s, b), (mm_o, a), (mm_s, c), (mm_o, b), (mm_o, c), (mm_s, slot), (mm_o, slot)):
+            f(s)
+
+        ve.memset(T.zero[:, :], 0.0).then_inc(sem.zs, 1)
+        ve.wait_ge(sem.zs, 1)
+        for f, s in ((relu, a), (relu, b), (out, a), (relu, c), (out, b), (out, c), (relu, slot)):
+            f(s)
+        oj = 1 - myj
+        ve.wait_ge(sem["om%d" % slot], 1)
+        ve.wait_ge(sem["pa%d" % oj], _count(both(cores[hubs[oj]], [core])))
+        ve.tensor_tensor(T.ybuf[:, 0:W], T["po%d" % slot][:, 0:W], cols(T.land, oj, W), AluOpType.add) \
+            .then_inc(sem.fin, 1)
+
+        for s in away:
+            dst = cores[mine[s]]
+            m = both(core, [dst])
+            rid, pid = topo.addr(dst)[0], topo.addr(dst)[1]
+            g.wait_ge(sem["cp%d" % s], 1)
+            g.remote_dma(cols(T.land, myj, bw[s]), cols(T.obuf, s, bw[s]), sem["pa%d" % myj], sem.snt, pid, rid, m)
+            sent += _count(m)
+
+    g.sync.wait_ge(sem.fin, 1)
+    g.sync.dma_start(T.y[:, 0:W], T.ybuf[:, 0:W]).then_inc(sem.st, 16)
+    g.sync.wait_ge(sem.st, 16)
+    g.wait_ge(sem.snt, sent)

@@ -1,40 +1,33 @@
-from concourse.bass import DstId, RemoteDMATransfer
 from concourse.mybir import AluOpType
 
 QP = 256
 KP = 128
-NB = 4
+NJ = 5
 
 SCRATCH = {
-    "kv": ("sbuf", [128, 2 * KP], "bfloat16"),
-    "qall": ("sbuf", [128, NB * QP], "bfloat16"),
+    "kv": ("sbuf", [128, 4 * KP], "bfloat16"),
+    "qown": ("sbuf", [128, QP], "bfloat16"),
+    "qoth": ("sbuf", [128, QP], "bfloat16"),
     "zero": ("sbuf", [128, QP], "float32"),
-    "srel": ("sbuf", [128, NB * QP], "bfloat16"),
-    "obuf": ("sbuf", [128, NB * QP], "bfloat16"),
-    "land": ("sbuf", [128, 2 * QP], "bfloat16"),
+    "srel": ("sbuf", [128, NJ * QP], "bfloat16"),
+    "obuf": ("sbuf", [128, QP], "bfloat16"),
+    "land": ("sbuf", [128, QP], "bfloat16"),
     "ybuf": ("sbuf", [128, QP], "bfloat16"),
 }
-for _b in range(NB):
-    SCRATCH["ps%d" % _b] = ("psum", [128, 512], "float32")
-    SCRATCH["po%d" % _b] = ("psum", [128, 512], "float32")
+for _b in range(8):
+    SCRATCH["bk%d" % _b] = ("psum", [128, 512], "float32")
 
-SEMAPHORES = ["ldkv", "ldq", "kva", "pa0", "pa1", "zs", "fin", "st", "snt"]
-for _b in range(NB):
-    SEMAPHORES += ["qa%d" % _b, "sm%d" % _b, "rl%d" % _b, "om%d" % _b, "cp%d" % _b]
+SEMAPHORES = ["ldkv", "ldq", "kva0", "kva1", "qa", "pa", "zs", "cp0", "cp1", "fin0", "fin1", "st", "snt"]
+for _b in range(NJ):
+    SEMAPHORES += ["sm%d" % _b, "rl%d" % _b, "om%d" % _b]
 
 
 def _count(m):
     return bin(m).count("1")
 
 
-def _low(m, n):
-    out, i = 0, 0
-    while n > 0:
-        if (m >> i) & 1:
-            out |= 1 << i
-            n -= 1
-        i += 1
-    return out
+def _halves(w):
+    return [(0, w)] if w < KP else [(0, w // 2), (w // 2, w)]
 
 
 def _plan(T, topo):
@@ -53,11 +46,15 @@ def _plan(T, topo):
         first = [ch for ch in chips if ch in home and ch != home[ji]]
         k = ji % len(plain) if plain else 0
         order.append(first + plain[k:] + plain[:k])
+
+    def turn(ji, ch):
+        return -1 if home[ji] == ch else order[ji].index(ch)
+
     hub = {}
     for ch in chips:
         h = [mem[ji] if home[ji] == ch else None for ji in range(len(mem))]
         free = sorted([r for r in members[ch] if r not in mem], key=lambda r: -wid[r])
-        todo = sorted([ji for ji in range(len(mem)) if h[ji] is None], key=lambda ji: -order[ji].index(ch))
+        todo = sorted([ji for ji in range(len(mem)) if h[ji] is None], key=lambda ji: -turn(ji, ch))
         for ji, r in zip(todo, free):
             h[ji] = r
         hub[ch] = h
@@ -75,18 +72,14 @@ def _plan(T, topo):
     def kv_mask(ji):
         return both(cores[mem[ji]], kv_dsts(ji))
 
-    def q_dsts(r):
-        return [cores[h] for h in hub[topo.chip(cores[r])] if h != r]
-
-    def q_mask(r):
-        full = both(cores[r], q_dsts(r))
-        if r in mem:
+    def chip_mask(r, early):
+        ch = topo.chip(cores[r])
+        full = both(cores[r], [cores[x] for x in members[ch] if x != r])
+        if early and r in mem:
             return full & ~kv_mask(mem.index(r))
-        if r in hub[topo.chip(cores[r])]:
-            return full
-        return _low(full, _count(full) // 2)
+        return full
 
-    return members, hub, kv_dsts, kv_mask, q_dsts, q_mask, both
+    return members, hub, turn, kv_dsts, kv_mask, chip_mask
 
 
 def rank_program(g, core, T, topo):
@@ -94,98 +87,141 @@ def rank_program(g, core, T, topo):
     if rank is None:
         return
     cores, wid, mem = T.cores, T.tables["WID"], T.tables["MEM"]
-    members, hub, kv_dsts, kv_mask, q_dsts, q_mask, both = _plan(T, topo)
+    members, hub, turn, kv_dsts, kv_mask, chip_mask = _plan(T, topo)
     sem = T.sem
-    mine = members[topo.chip(core)]
-    hubs = hub[topo.chip(core)]
-    slot, W = mine.index(rank), wid[rank]
+    chip = topo.chip(core)
+    mine, hubs = members[chip], hub[chip]
+    W = wid[rank]
     is_mem = rank in mem
     myj = hubs.index(rank) if rank in hubs else None
-
-    def cols(t, s, w):
-        return t[:, s * QP:s * QP + w]
-
-    def ids(dsts):
-        return [DstId(rid=topo.addr(d)[0], pnc=topo.addr(d)[1]) for d in dsts]
-
-    if is_mem:
-        g.sync.dma_start(T.kv[:, 0:KP], T.k[:, :]).then_inc(sem.ldkv, 16)
-        g.scalar.dma_start(T.kv[:, KP:2 * KP], T.v[:, :]).then_inc(sem.ldkv, 16)
-    g.sync.dma_start(cols(T.qall, slot, W), T.q[:, 0:W]).then_inc(sem.ldq, 16)
-
-    sent = 0
-    if is_mem:
-        ji = mem.index(rank)
-        d = kv_dsts(ji)
-        g.wait_ge(sem.ldkv, 32)
-        g.remote_dma_fused([RemoteDMATransfer(dst_ids=ids(d), dma_engine_mask=kv_mask(ji), remote_sem=sem.kva,
-                                              srcs=[T.kv[:, :]], dsts=[T.kv[:, :] for _ in d])], local_sem=sem.snt)
-        sent += _count(kv_mask(ji))
-    d = q_dsts(rank)
-    g.wait_ge(sem.ldq, 16)
-    g.remote_dma_fused([RemoteDMATransfer(dst_ids=ids(d), dma_engine_mask=q_mask(rank), remote_sem=sem["qa%d" % slot],
-                                          srcs=[cols(T.qall, slot, W)], dsts=[cols(T.qall, slot, W) for _ in d])],
-                       local_sem=sem.snt)
-    sent += _count(q_mask(rank))
-
+    sent = [0]
     te, ve = g.tensor, g.vector
-    if myj is None:
-        for ji in range(len(mem)):
-            ve.wait_ge(sem["pa%d" % ji], _count(both(cores[hubs[ji]], [core])))
-        ve.tensor_tensor(T.ybuf[:, 0:W], cols(T.land, 0, W), cols(T.land, 1, W), AluOpType.add).then_inc(sem.fin, 1)
-    else:
-        away = sorted([s for s in range(len(mine)) if s != slot], key=lambda s: -wid[mine[s]])
-        bw = {s: wid[mine[s]] for s in range(len(mine))}
 
-        def mm_s(s):
-            if s == slot:
-                te.wait_ge(sem.ldq, 16)
+    def kvs(ji):
+        return T.kv[:, 2 * KP * ji:2 * KP * (ji + 1)]
+
+    def write(dst, out_ap, in_ap, rsem, mask):
+        g.remote_dma(out_ap, in_ap, rsem, sem.snt, topo.addr(dst)[1], topo.addr(dst)[0], mask)
+        sent[0] += _count(mask)
+
+    def jobs(first_id, ji, q, w, sbank, obank, start, stop):
+        return [(first_id + n, ji, q, c0, c1, T["bk%d" % (sbank + n)], T["bk%d" % (obank + n)], start, stop)
+                for n, (c0, c1) in enumerate(_halves(w))]
+
+    def mm_s(js):
+        for i, ji, q, c0, c1, sb, ob, start, stop in js:
+            te.matmul(sb[:, 0:c1 - c0], T.kv[:, 2 * KP * ji:2 * KP * ji + KP], q[:, c0:c1], True, True) \
+                .then_inc(sem["sm%d" % i], 1)
+
+    def mm_o(js):
+        for i, ji, q, c0, c1, sb, ob, start, stop in js:
+            te.wait_ge(sem["rl%d" % i], 1)
+            ins = te.matmul(ob[:, 0:c1 - c0], T.kv[:, 2 * KP * ji + KP:2 * KP * (ji + 1)],
+                            T.srel[:, i * QP:i * QP + c1 - c0], start, stop)
+            if stop:
+                ins.then_inc(sem["om%d" % i], 1)
+
+    def relu(js):
+        for i, ji, q, c0, c1, sb, ob, start, stop in js:
+            ve.wait_ge(sem["sm%d" % i], 1)
+            ve.tensor_tensor(T.srel[:, i * QP:i * QP + c1 - c0], sb[:, 0:c1 - c0], T.zero[:, 0:c1 - c0],
+                             AluOpType.max).then_inc(sem["rl%d" % i], 1)
+
+    def out(js, dst, done, plus=None):
+        for n, (i, ji, q, c0, c1, sb, ob, start, stop) in enumerate(js):
+            ve.wait_ge(sem["om%d" % i], 1)
+            if plus is None:
+                ins = ve.tensor_copy(dst[:, c0:c1], ob[:, 0:c1 - c0])
             else:
-                te.wait_ge(sem["qa%d" % s], _count(q_mask(mine[s])))
-            te.matmul(T["ps%d" % s][:, 0:bw[s]], T.kv[:, 0:KP], cols(T.qall, s, bw[s]), True, True) \
-                .then_inc(sem["sm%d" % s], 1)
+                ins = ve.tensor_tensor(dst[:, c0:c1], ob[:, 0:c1 - c0], plus[:, c0:c1], AluOpType.add)
+            ins.then_inc(sem["%s%d" % (done, n)], 1)
 
-        def mm_o(s):
-            te.wait_ge(sem["rl%d" % s], 1)
-            te.matmul(T["po%d" % s][:, 0:bw[s]], T.kv[:, KP:2 * KP], cols(T.srel, s, bw[s]), True, True) \
-                .then_inc(sem["om%d" % s], 1)
+    if is_mem:
+        g.sync.dma_start(T.kv[:, 2 * KP * myj:2 * KP * myj + KP], T.k[:, :]).then_inc(sem.ldkv, 16)
+        g.scalar.dma_start(T.kv[:, 2 * KP * myj + KP:2 * KP * (myj + 1)], T.v[:, :]).then_inc(sem.ldkv, 16)
+    g.sync.dma_start(T.qown[:, 0:W], T.q[:, 0:W]).then_inc(sem.ldq, 16)
+    ve.memset(T.zero[:, :], 0.0).then_inc(sem.zs, 1)
+    ve.wait_ge(sem.zs, 1)
 
-        def relu(s):
-            ve.wait_ge(sem["sm%d" % s], 1)
-            ve.tensor_tensor(cols(T.srel, s, bw[s]), T["ps%d" % s][:, 0:bw[s]], T.zero[:, 0:bw[s]], AluOpType.max) \
-                .then_inc(sem["rl%d" % s], 1)
+    leaves = sorted([r for r in mine if r not in hubs], key=lambda r: -wid[r])
+    with_mem = any(h in mem for h in hubs)
 
-        def out(s):
-            ve.wait_ge(sem["om%d" % s], 1)
-            ve.tensor_copy(cols(T.obuf, s, bw[s]), T["po%d" % s][:, 0:bw[s]]).then_inc(sem["cp%d" % s], 1)
-
-        if is_mem:
-            te.wait_ge(sem.ldkv, 32)
-        else:
-            te.wait_ge(sem.kva, _count(kv_mask(myj)))
-        a, b, c = away
-        for f, s in ((mm_s, a), (mm_s, b), (mm_o, a), (mm_s, c), (mm_o, b), (mm_o, c), (mm_s, slot), (mm_o, slot)):
-            f(s)
-
-        ve.memset(T.zero[:, :], 0.0).then_inc(sem.zs, 1)
-        ve.wait_ge(sem.zs, 1)
-        for f, s in ((relu, a), (relu, b), (out, a), (relu, c), (out, b), (out, c), (relu, slot)):
-            f(s)
+    if myj is None:
+        e, l = sorted(range(len(mem)), key=lambda ji: turn(ji, chip))
+        je = jobs(0, e, T.qown, W, 0, 4, True, False)
+        jl = jobs(2, l, T.qown, W, 2, 4, False, True)
+        te.wait_ge(sem.ldq, 16)
+        for ji, js in ((e, je), (l, jl)):
+            te.wait_ge(sem["kva%d" % ji], _count(chip_mask(hubs[ji], True)))
+            mm_s(js)
+            mm_o(js)
+        relu(je)
+        relu(jl)
+        out(jl, T.ybuf, "fin")
+    elif is_mem:
         oj = 1 - myj
-        ve.wait_ge(sem["om%d" % slot], 1)
-        ve.wait_ge(sem["pa%d" % oj], _count(both(cores[hubs[oj]], [core])))
-        ve.tensor_tensor(T.ybuf[:, 0:W], T["po%d" % slot][:, 0:W], cols(T.land, oj, W), AluOpType.add) \
-            .then_inc(sem.fin, 1)
+        other = hubs[oj]
+        Wo = wid[other]
+        g.wait_ge(sem.ldkv, 32)
+        for d in kv_dsts(myj):
+            write(d, kvs(myj), kvs(myj), sem["kva%d" % myj], kv_mask(myj))
+        for r in leaves:
+            write(cores[r], kvs(myj), kvs(myj), sem["kva%d" % myj], chip_mask(rank, True))
+        g.wait_ge(sem.cp0, 1)
+        write(cores[other], T.land[:, 0:Wo], T.obuf[:, 0:Wo], sem.pa, chip_mask(rank, False))
 
-        for s in away:
-            dst = cores[mine[s]]
-            m = both(core, [dst])
-            rid, pid = topo.addr(dst)[0], topo.addr(dst)[1]
-            g.wait_ge(sem["cp%d" % s], 1)
-            g.remote_dma(cols(T.land, myj, bw[s]), cols(T.obuf, s, bw[s]), sem["pa%d" % myj], sem.snt, pid, rid, m)
-            sent += _count(m)
+        je = jobs(0, myj, T.qown, W, 0, 4, True, False)
+        jl = jobs(2, oj, T.qown, W, 2, 4, False, True)
+        jx = [(4, myj, T.qoth, 0, Wo, T.bk6, T.bk7, True, True)]
+        te.wait_ge(sem.ldkv, 32)
+        te.wait_ge(sem.ldq, 16)
+        mm_s(je)
+        mm_o(je)
+        te.wait_ge(sem.qa, _count(chip_mask(other, True)))
+        mm_s(jx)
+        mm_o(jx)
+        te.wait_ge(sem["kva%d" % oj], _count(chip_mask(other, True)))
+        mm_s(jl)
+        mm_o(jl)
+        relu(je)
+        relu(jx)
+        out(jx, T.obuf, "cp")
+        relu(jl)
+        out(jl, T.ybuf, "fin")
+    else:
+        other = hubs[1 - myj]
+        Wo = wid[other]
+        kva, nkv = sem["kva%d" % myj], _count(kv_mask(myj))
+        jo = jobs(2, myj, T.qown, W, 2, 6, True, True)
+        ja = [] if with_mem else jobs(0, myj, T.qoth, Wo, 0, 4, True, True)
 
-    g.sync.wait_ge(sem.fin, 1)
+        g.wait_ge(sem.ldq, 16)
+        write(cores[other], T.qoth[:, 0:W], T.qown[:, 0:W], sem.qa, chip_mask(rank, True))
+        g.wait_ge(kva, nkv)
+        for r in ([other] if with_mem else []) + leaves:
+            write(cores[r], kvs(myj), kvs(myj), kva, chip_mask(rank, True))
+        if ja:
+            for n in range(len(ja)):
+                g.wait_ge(sem["cp%d" % n], 1)
+            write(cores[other], T.land[:, 0:Wo], T.obuf[:, 0:Wo], sem.pa, chip_mask(rank, False))
+
+        te.wait_ge(kva, nkv)
+        if ja:
+            te.wait_ge(sem.qa, _count(chip_mask(other, True)))
+            mm_s(ja)
+            mm_o(ja)
+        te.wait_ge(sem.ldq, 16)
+        mm_s(jo)
+        mm_o(jo)
+        relu(ja)
+        out(ja, T.obuf, "cp")
+        relu(jo)
+        ve.wait_ge(sem.pa, _count(chip_mask(other, False)))
+        out(jo, T.ybuf, "fin", T.land)
+
+    for n in range(len(_halves(W))):
+        g.sync.wait_ge(sem["fin%d" % n], 1)
     g.sync.dma_start(T.y[:, 0:W], T.ybuf[:, 0:W]).then_inc(sem.st, 16)
     g.sync.wait_ge(sem.st, 16)
-    g.wait_ge(sem.snt, sent)
+    if sent[0]:
+        g.wait_ge(sem.snt, sent[0])

@@ -1,3 +1,4 @@
+from concourse.bass import DstId, RemoteDMATransfer
 from concourse.mybir import AluOpType
 
 QP = 256
@@ -6,6 +7,7 @@ NJ = 5
 
 SCRATCH = {
     "kv": ("sbuf", [128, 4 * KP], "bfloat16"),
+    "kvd": ("dram", [4, 128, KP], "bfloat16"),
     "qown": ("sbuf", [128, QP], "bfloat16"),
     "qoth": ("sbuf", [128, QP], "bfloat16"),
     "zero": ("sbuf", [128, QP], "float32"),
@@ -17,7 +19,8 @@ SCRATCH = {
 for _b in range(8):
     SCRATCH["bk%d" % _b] = ("psum", [128, 512], "float32")
 
-SEMAPHORES = ["ldkv", "ldq", "kva0", "kva1", "qa", "pa", "zs", "cp0", "cp1", "fin0", "fin1", "st", "snt"]
+SEMAPHORES = ["ldk", "ldv", "ldkd", "ldvd", "ldq", "ka0", "ka1", "va0", "va1", "qa", "pa0", "pa1", "zs", "cp0", "cp1",
+              "fin0", "fin1", "st0", "st1", "snt"]
 for _b in range(NJ):
     SEMAPHORES += ["sm%d" % _b, "rl%d" % _b, "om%d" % _b]
 
@@ -66,16 +69,16 @@ def _plan(T, topo):
             m &= topo.mask(src, d)
         return m
 
-    def kv_dsts(ji):
-        return [cores[hub[ch][ji]] for ch in order[ji]]
+    def kv_dsts(ji, with_mem):
+        return [cores[hub[ch][ji]] for ch in order[ji] if (ch in home) == with_mem]
 
     def kv_mask(ji):
-        return both(cores[mem[ji]], kv_dsts(ji))
+        return both(cores[mem[ji]], kv_dsts(ji, True) + kv_dsts(ji, False))
 
-    def chip_mask(r, early):
+    def chip_mask(r):
         ch = topo.chip(cores[r])
         full = both(cores[r], [cores[x] for x in members[ch] if x != r])
-        if early and r in mem:
+        if r in mem:
             return full & ~kv_mask(mem.index(r))
         return full
 
@@ -97,12 +100,32 @@ def rank_program(g, core, T, topo):
     sent = [0]
     te, ve = g.tensor, g.vector
 
+    def ks(ji):
+        return T.kv[:, 2 * KP * ji:2 * KP * ji + KP]
+
+    def vs(ji):
+        return T.kv[:, 2 * KP * ji + KP:2 * KP * (ji + 1)]
+
     def kvs(ji):
         return T.kv[:, 2 * KP * ji:2 * KP * (ji + 1)]
 
-    def write(dst, out_ap, in_ap, rsem, mask):
-        g.remote_dma(out_ap, in_ap, rsem, sem.snt, topo.addr(dst)[1], topo.addr(dst)[0], mask)
+    def write(dsts, out_ap, in_ap, rsem, mask):
+        if len(dsts) == 1:
+            g.remote_dma(out_ap, in_ap, rsem, sem.snt, topo.addr(dsts[0])[1], topo.addr(dsts[0])[0], mask)
+        else:
+            ids = [DstId(rid=topo.addr(d)[0], pnc=topo.addr(d)[1]) for d in dsts]
+            g.remote_dma_fused([RemoteDMATransfer(dst_ids=ids, dma_engine_mask=mask, remote_sem=rsem,
+                                                  srcs=[in_ap], dsts=[out_ap for d in dsts])], local_sem=sem.snt)
         sent[0] += _count(mask)
+
+    def arrived(queue, ji, part):
+        h = hubs[ji]
+        if h == rank:
+            queue.wait_ge(sem["%s%d" % (part, ji)], _count(kv_mask(ji)))
+        elif h in mem:
+            queue.wait_ge(sem["ka%d" % ji], _count(chip_mask(h)))
+        else:
+            queue.wait_ge(sem["%s%d" % (part, ji)], _count(chip_mask(h)))
 
     def jobs(first_id, ji, q, w, sbank, obank, start, stop):
         return [(first_id + n, ji, q, c0, c1, T["bk%d" % (sbank + n)], T["bk%d" % (obank + n)], start, stop)
@@ -110,14 +133,12 @@ def rank_program(g, core, T, topo):
 
     def mm_s(js):
         for i, ji, q, c0, c1, sb, ob, start, stop in js:
-            te.matmul(sb[:, 0:c1 - c0], T.kv[:, 2 * KP * ji:2 * KP * ji + KP], q[:, c0:c1], True, True) \
-                .then_inc(sem["sm%d" % i], 1)
+            te.matmul(sb[:, 0:c1 - c0], ks(ji), q[:, c0:c1], True, True).then_inc(sem["sm%d" % i], 1)
 
     def mm_o(js):
         for i, ji, q, c0, c1, sb, ob, start, stop in js:
             te.wait_ge(sem["rl%d" % i], 1)
-            ins = te.matmul(ob[:, 0:c1 - c0], T.kv[:, 2 * KP * ji + KP:2 * KP * (ji + 1)],
-                            T.srel[:, i * QP:i * QP + c1 - c0], start, stop)
+            ins = te.matmul(ob[:, 0:c1 - c0], vs(ji), T.srel[:, i * QP:i * QP + c1 - c0], start, stop)
             if stop:
                 ins.then_inc(sem["om%d" % i], 1)
 
@@ -127,18 +148,23 @@ def rank_program(g, core, T, topo):
             ve.tensor_tensor(T.srel[:, i * QP:i * QP + c1 - c0], sb[:, 0:c1 - c0], T.zero[:, 0:c1 - c0],
                              AluOpType.max).then_inc(sem["rl%d" % i], 1)
 
-    def out(js, dst, done, plus=None):
+    def out(js, dst, done, plus=None, landed=0, pieces=1):
         for n, (i, ji, q, c0, c1, sb, ob, start, stop) in enumerate(js):
             ve.wait_ge(sem["om%d" % i], 1)
             if plus is None:
                 ins = ve.tensor_copy(dst[:, c0:c1], ob[:, 0:c1 - c0])
             else:
+                if n < pieces:
+                    ve.wait_ge(sem["pa%d" % n], landed)
                 ins = ve.tensor_tensor(dst[:, c0:c1], ob[:, 0:c1 - c0], plus[:, c0:c1], AluOpType.add)
             ins.then_inc(sem["%s%d" % (done, n)], 1)
 
     if is_mem:
-        g.sync.dma_start(T.kv[:, 2 * KP * myj:2 * KP * myj + KP], T.k[:, :]).then_inc(sem.ldkv, 16)
-        g.scalar.dma_start(T.kv[:, 2 * KP * myj + KP:2 * KP * (myj + 1)], T.v[:, :]).then_inc(sem.ldkv, 16)
+        g.sync.dma_start(T.kvd[2 * myj], T.k[:, :]).then_inc(sem.ldkd, 16)
+        g.sync.dma_start(ks(myj), T.k[:, :]).then_inc(sem.ldk, 16)
+        g.scalar.wait_ge(sem.ldkd, 16)
+        g.scalar.dma_start(T.kvd[2 * myj + 1], T.v[:, :]).then_inc(sem.ldvd, 16)
+        g.scalar.dma_start(vs(myj), T.v[:, :]).then_inc(sem.ldv, 16)
     g.sync.dma_start(T.qown[:, 0:W], T.q[:, 0:W]).then_inc(sem.ldq, 16)
     ve.memset(T.zero[:, :], 0.0).then_inc(sem.zs, 1)
     ve.wait_ge(sem.zs, 1)
@@ -151,10 +177,14 @@ def rank_program(g, core, T, topo):
         je = jobs(0, e, T.qown, W, 0, 4, True, False)
         jl = jobs(2, l, T.qown, W, 2, 4, False, True)
         te.wait_ge(sem.ldq, 16)
-        for ji, js in ((e, je), (l, jl)):
-            te.wait_ge(sem["kva%d" % ji], _count(chip_mask(hubs[ji], True)))
-            mm_s(js)
-            mm_o(js)
+        arrived(te, e, "ka")
+        mm_s(je)
+        arrived(te, l, "ka")
+        mm_s(jl)
+        arrived(te, e, "va")
+        mm_o(je)
+        arrived(te, l, "va")
+        mm_o(jl)
         relu(je)
         relu(jl)
         out(jl, T.ybuf, "fin")
@@ -162,26 +192,34 @@ def rank_program(g, core, T, topo):
         oj = 1 - myj
         other = hubs[oj]
         Wo = wid[other]
-        g.wait_ge(sem.ldkv, 32)
-        for d in kv_dsts(myj):
-            write(d, kvs(myj), kvs(myj), sem["kva%d" % myj], kv_mask(myj))
-        for r in leaves:
-            write(cores[r], kvs(myj), kvs(myj), sem["kva%d" % myj], chip_mask(rank, True))
+        ka, va = sem["ka%d" % myj], sem["va%d" % myj]
+        kd, vd = T.kvd[2 * myj], T.kvd[2 * myj + 1]
+        g.wait_ge(sem.ldkd, 16)
+        write(kv_dsts(myj, False), ks(myj), kd, ka, kv_mask(myj))
+        write(kv_dsts(myj, True), kd, kd, ka, kv_mask(myj))
+        g.wait_ge(sem.ldvd, 16)
+        write(kv_dsts(myj, True), vd, vd, va, kv_mask(myj))
+        write(kv_dsts(myj, False), vs(myj), vd, va, kv_mask(myj))
+        g.wait_ge(sem.ldk, 16)
+        g.wait_ge(sem.ldv, 16)
+        write([cores[r] for r in leaves], kvs(myj), kvs(myj), ka, chip_mask(rank))
         g.wait_ge(sem.cp0, 1)
-        write(cores[other], T.land[:, 0:Wo], T.obuf[:, 0:Wo], sem.pa, chip_mask(rank, False))
+        write([cores[other]], T.land[:, 0:Wo], T.obuf[:, 0:Wo], sem.pa0, chip_mask(rank))
 
         je = jobs(0, myj, T.qown, W, 0, 4, True, False)
         jl = jobs(2, oj, T.qown, W, 2, 4, False, True)
         jx = [(4, myj, T.qoth, 0, Wo, T.bk6, T.bk7, True, True)]
-        te.wait_ge(sem.ldkv, 32)
+        te.wait_ge(sem.ldk, 16)
+        te.wait_ge(sem.ldv, 16)
         te.wait_ge(sem.ldq, 16)
         mm_s(je)
         mm_o(je)
-        te.wait_ge(sem.qa, _count(chip_mask(other, True)))
+        te.wait_ge(sem.qa, _count(chip_mask(other)))
         mm_s(jx)
         mm_o(jx)
-        te.wait_ge(sem["kva%d" % oj], _count(chip_mask(other, True)))
+        arrived(te, oj, "ka")
         mm_s(jl)
+        arrived(te, oj, "va")
         mm_o(jl)
         relu(je)
         relu(jx)
@@ -191,37 +229,52 @@ def rank_program(g, core, T, topo):
     else:
         other = hubs[1 - myj]
         Wo = wid[other]
-        kva, nkv = sem["kva%d" % myj], _count(kv_mask(myj))
         jo = jobs(2, myj, T.qown, W, 2, 6, True, True)
         ja = [] if with_mem else jobs(0, myj, T.qoth, Wo, 0, 4, True, True)
+        served = ([other] if with_mem else []) + leaves
+        ksrc = T.kvd[2 * myj] if with_mem else ks(myj)
+        vsrc = T.kvd[2 * myj + 1] if with_mem else vs(myj)
 
         g.wait_ge(sem.ldq, 16)
-        write(cores[other], T.qoth[:, 0:W], T.qown[:, 0:W], sem.qa, chip_mask(rank, True))
-        g.wait_ge(kva, nkv)
-        for r in ([other] if with_mem else []) + leaves:
-            write(cores[r], kvs(myj), kvs(myj), kva, chip_mask(rank, True))
-        if ja:
-            for n in range(len(ja)):
-                g.wait_ge(sem["cp%d" % n], 1)
-            write(cores[other], T.land[:, 0:Wo], T.obuf[:, 0:Wo], sem.pa, chip_mask(rank, False))
+        write([cores[other]], T.qoth[:, 0:W], T.qown[:, 0:W], sem.qa, chip_mask(rank))
+        arrived(g, myj, "ka")
+        write([cores[r] for r in served], ks(myj), ksrc, sem["ka%d" % myj], chip_mask(rank))
+        arrived(g, myj, "va")
+        write([cores[r] for r in served], vs(myj), vsrc, sem["va%d" % myj], chip_mask(rank))
+        for n, job in enumerate(ja):
+            g.wait_ge(sem["cp%d" % n], 1)
+            write([cores[other]], T.land[:, job[3]:job[4]], T.obuf[:, job[3]:job[4]], sem["pa%d" % n],
+                  chip_mask(rank))
 
-        te.wait_ge(kva, nkv)
+        if with_mem:
+            arrived(g.sync, myj, "ka")
+            g.sync.dma_start(ks(myj), ksrc).then_inc(sem.ldk, 16)
+            arrived(g.scalar, myj, "va")
+            g.scalar.dma_start(vs(myj), vsrc).then_inc(sem.ldv, 16)
+            te.wait_ge(sem.ldk, 16)
+        else:
+            arrived(te, myj, "ka")
         if ja:
-            te.wait_ge(sem.qa, _count(chip_mask(other, True)))
+            te.wait_ge(sem.qa, _count(chip_mask(other)))
             mm_s(ja)
-            mm_o(ja)
         te.wait_ge(sem.ldq, 16)
         mm_s(jo)
+        if with_mem:
+            te.wait_ge(sem.ldv, 16)
+        else:
+            arrived(te, myj, "va")
+        mm_o(ja)
         mm_o(jo)
         relu(ja)
-        out(ja, T.obuf, "cp")
         relu(jo)
-        ve.wait_ge(sem.pa, _count(chip_mask(other, False)))
-        out(jo, T.ybuf, "fin", T.land)
+        out(ja, T.obuf, "cp")
+        out(jo, T.ybuf, "fin", T.land, _count(chip_mask(other)), 1 if with_mem else len(jo))
 
-    for n in range(len(_halves(W))):
-        g.sync.wait_ge(sem["fin%d" % n], 1)
-    g.sync.dma_start(T.y[:, 0:W], T.ybuf[:, 0:W]).then_inc(sem.st, 16)
-    g.sync.wait_ge(sem.st, 16)
+    hs = _halves(W)
+    for n, (c0, c1) in enumerate(hs):
+        qu = g.sync if n == len(hs) - 1 else g.scalar
+        qu.wait_ge(sem["fin%d" % n], 1)
+        qu.dma_start(T.y[:, c0:c1], T.ybuf[:, c0:c1]).then_inc(sem["st%d" % n], 16)
+        qu.wait_ge(sem["st%d" % n], 16)
     if sent[0]:
         g.wait_ge(sem.snt, sent[0])

from concourse.bass import DstId, RemoteDMATransfer
from concourse.mybir import AluOpType

QP = 256
KP = 128
NJ = 5

SCRATCH = {
    "kv": ("sbuf", [128, 4 * KP], "bfloat16"),
    "kvd": ("dram", [4, 128, KP], "bfloat16"),
    "qown": ("sbuf", [128, QP], "bfloat16"),
    "qoth": ("sbuf", [128, QP], "bfloat16"),
    "zero": ("sbuf", [128, QP], "float32"),
    "srel": ("sbuf", [128, NJ * QP], "bfloat16"),
    "obuf": ("sbuf", [128, QP], "bfloat16"),
    "land": ("sbuf", [128, QP], "bfloat16"),
    "ybuf": ("sbuf", [128, QP], "bfloat16"),
}
for _b in range(8):
    SCRATCH["bk%d" % _b] = ("psum", [128, 512], "float32")

SEMAPHORES = ["ldk", "ldv", "ldkd", "ldvd", "ldq", "ka0", "ka1", "va0", "va1", "qa", "pa0", "pa1", "zs", "cp0", "cp1",
              "fin0", "fin1", "st0", "st1", "snt"]
for _b in range(NJ):
    SEMAPHORES += ["sm%d" % _b, "rl%d" % _b, "om%d" % _b]


def _count(m):
    return bin(m).count("1")


def _halves(w):
    return [(0, w)] if w < KP else [(0, w // 2), (w // 2, w)]


def _plan(T, topo):
    cores, wid, mem = T.cores, T.tables["WID"], T.tables["MEM"]
    chips, members = [], {}
    for r, c in enumerate(cores):
        ch = topo.chip(c)
        if ch not in members:
            members[ch] = []
            chips.append(ch)
        members[ch].append(r)
    home = [topo.chip(cores[m]) for m in mem]
    plain = [ch for ch in chips if ch not in home]
    order = []
    for ji in range(len(mem)):
        first = [ch for ch in chips if ch in home and ch != home[ji]]
        k = ji % len(plain) if plain else 0
        order.append(first + plain[k:] + plain[:k])

    def turn(ji, ch):
        return -1 if home[ji] == ch else order[ji].index(ch)

    hub = {}
    for ch in chips:
        h = [mem[ji] if home[ji] == ch else None for ji in range(len(mem))]
        free = sorted([r for r in members[ch] if r not in mem], key=lambda r: -wid[r])
        todo = sorted([ji for ji in range(len(mem)) if h[ji] is None], key=lambda ji: -turn(ji, ch))
        for ji, r in zip(todo, free):
            h[ji] = r
        hub[ch] = h

    def both(src, dsts):
        m = topo.mask(src, dsts[0])
        for d in dsts:
            assert topo.may_write(src, d)
            m &= topo.mask(src, d)
        return m

    def kv_dsts(ji, with_mem):
        return [cores[hub[ch][ji]] for ch in order[ji] if (ch in home) == with_mem]

    def kv_mask(ji):
        return both(cores[mem[ji]], kv_dsts(ji, True) + kv_dsts(ji, False))

    def chip_mask(r):
        ch = topo.chip(cores[r])
        full = both(cores[r], [cores[x] for x in members[ch] if x != r])
        if r in mem:
            return full & ~kv_mask(mem.index(r))
        return full

    return members, hub, turn, kv_dsts, kv_mask, chip_mask


def rank_program(g, core, T, topo):
    rank = T.rank_of(core)
    if rank is None:
        return
    cores, wid, mem = T.cores, T.tables["WID"], T.tables["MEM"]
    members, hub, turn, kv_dsts, kv_mask, chip_mask = _plan(T, topo)
    sem = T.sem
    chip = topo.chip(core)
    mine, hubs = members[chip], hub[chip]
    W = wid[rank]
    is_mem = rank in mem
    myj = hubs.index(rank) if rank in hubs else None
    sent = [0]
    te, ve = g.tensor, g.vector

    def ks(ji):
        return T.kv[:, 2 * KP * ji:2 * KP * ji + KP]

    def vs(ji):
        return T.kv[:, 2 * KP * ji + KP:2 * KP * (ji + 1)]

    def kvs(ji):
        return T.kv[:, 2 * KP * ji:2 * KP * (ji + 1)]

    def write(dsts, out_ap, in_ap, rsem, mask):
        if len(dsts) == 1:
            g.remote_dma(out_ap, in_ap, rsem, sem.snt, topo.addr(dsts[0])[1], topo.addr(dsts[0])[0], mask)
        else:
            ids = [DstId(rid=topo.addr(d)[0], pnc=topo.addr(d)[1]) for d in dsts]
            g.remote_dma_fused([RemoteDMATransfer(dst_ids=ids, dma_engine_mask=mask, remote_sem=rsem,
                                                  srcs=[in_ap], dsts=[out_ap for d in dsts])], local_sem=sem.snt)
        sent[0] += _count(mask)

    def arrived(queue, ji, part):
        h = hubs[ji]
        if h == rank:
            queue.wait_ge(sem["%s%d" % (part, ji)], _count(kv_mask(ji)))
        elif h in mem:
            queue.wait_ge(sem["ka%d" % ji], _count(chip_mask(h)))
        else:
            queue.wait_ge(sem["%s%d" % (part, ji)], _count(chip_mask(h)))

    def jobs(first_id, ji, q, w, sbank, obank, start, stop):
        return [(first_id + n, ji, q, c0, c1, T["bk%d" % (sbank + n)], T["bk%d" % (obank + n)], start, stop)
                for n, (c0, c1) in enumerate(_halves(w))]

    def mm_s(js):
        for i, ji, q, c0, c1, sb, ob, start, stop in js:
            te.matmul(sb[:, 0:c1 - c0], ks(ji), q[:, c0:c1], True, True).then_inc(sem["sm%d" % i], 1)

    def mm_o(js):
        for i, ji, q, c0, c1, sb, ob, start, stop in js:
            te.wait_ge(sem["rl%d" % i], 1)
            ins = te.matmul(ob[:, 0:c1 - c0], vs(ji), T.srel[:, i * QP:i * QP + c1 - c0], start, stop)
            if stop:
                ins.then_inc(sem["om%d" % i], 1)

    def relu(js):
        for i, ji, q, c0, c1, sb, ob, start, stop in js:
            ve.wait_ge(sem["sm%d" % i], 1)
            ve.tensor_tensor(T.srel[:, i * QP:i * QP + c1 - c0], sb[:, 0:c1 - c0], T.zero[:, 0:c1 - c0],
                             AluOpType.max).then_inc(sem["rl%d" % i], 1)

    def out(js, dst, done, plus=None, landed=0, pieces=1):
        for n, (i, ji, q, c0, c1, sb, ob, start, stop) in enumerate(js):
            ve.wait_ge(sem["om%d" % i], 1)
            if plus is None:
                ins = ve.tensor_copy(dst[:, c0:c1], ob[:, 0:c1 - c0])
            else:
                if n < pieces:
                    ve.wait_ge(sem["pa%d" % n], landed)
                ins = ve.tensor_tensor(dst[:, c0:c1], ob[:, 0:c1 - c0], plus[:, c0:c1], AluOpType.add)
            ins.then_inc(sem["%s%d" % (done, n)], 1)

    if is_mem:
        g.sync.dma_start(T.kvd[2 * myj], T.k[:, :]).then_inc(sem.ldkd, 16)
        g.sync.dma_start(ks(myj), T.k[:, :]).then_inc(sem.ldk, 16)
        g.scalar.wait_ge(sem.ldkd, 16)
        g.scalar.dma_start(T.kvd[2 * myj + 1], T.v[:, :]).then_inc(sem.ldvd, 16)
        g.scalar.dma_start(vs(myj), T.v[:, :]).then_inc(sem.ldv, 16)
    g.sync.dma_start(T.qown[:, 0:W], T.q[:, 0:W]).then_inc(sem.ldq, 16)
    ve.memset(T.zero[:, :], 0.0).then_inc(sem.zs, 1)
    ve.wait_ge(sem.zs, 1)

    leaves = sorted([r for r in mine if r not in hubs], key=lambda r: -wid[r])
    with_mem = any(h in mem for h in hubs)

    if myj is None:
        e, l = sorted(range(len(mem)), key=lambda ji: turn(ji, chip))
        je = jobs(0, e, T.qown, W, 0, 4, True, False)
        jl = jobs(2, l, T.qown, W, 2, 4, False, True)
        te.wait_ge(sem.ldq, 16)
        arrived(te, e, "ka")
        mm_s(je)
        arrived(te, l, "ka")
        mm_s(jl)
        arrived(te, e, "va")
        mm_o(je)
        arrived(te, l, "va")
        mm_o(jl)
        relu(je)
        relu(jl)
        out(jl, T.ybuf, "fin")
    elif is_mem:
        oj = 1 - myj
        other = hubs[oj]
        Wo = wid[other]
        ka, va = sem["ka%d" % myj], sem["va%d" % myj]
        kd, vd = T.kvd[2 * myj], T.kvd[2 * myj + 1]
        g.wait_ge(sem.ldkd, 16)
        write(kv_dsts(myj, False), ks(myj), kd, ka, kv_mask(myj))
        write(kv_dsts(myj, True), kd, kd, ka, kv_mask(myj))
        g.wait_ge(sem.ldvd, 16)
        write(kv_dsts(myj, True), vd, vd, va, kv_mask(myj))
        write(kv_dsts(myj, False), vs(myj), vd, va, kv_mask(myj))
        g.wait_ge(sem.ldk, 16)
        g.wait_ge(sem.ldv, 16)
        write([cores[r] for r in leaves], kvs(myj), kvs(myj), ka, chip_mask(rank))
        g.wait_ge(sem.cp0, 1)
        write([cores[other]], T.land[:, 0:Wo], T.obuf[:, 0:Wo], sem.pa0, chip_mask(rank))

        je = jobs(0, myj, T.qown, W, 0, 4, True, False)
        jl = jobs(2, oj, T.qown, W, 2, 4, False, True)
        jx = [(4, myj, T.qoth, 0, Wo, T.bk6, T.bk7, True, True)]
        te.wait_ge(sem.ldk, 16)
        te.wait_ge(sem.ldv, 16)
        te.wait_ge(sem.ldq, 16)
        mm_s(je)
        mm_o(je)
        te.wait_ge(sem.qa, _count(chip_mask(other)))
        mm_s(jx)
        mm_o(jx)
        arrived(te, oj, "ka")
        mm_s(jl)
        arrived(te, oj, "va")
        mm_o(jl)
        relu(je)
        relu(jx)
        out(jx, T.obuf, "cp")
        relu(jl)
        out(jl, T.ybuf, "fin")
    else:
        other = hubs[1 - myj]
        Wo = wid[other]
        jo = jobs(2, myj, T.qown, W, 2, 6, True, True)
        ja = [] if with_mem else jobs(0, myj, T.qoth, Wo, 0, 4, True, True)
        served = ([other] if with_mem else []) + leaves
        ksrc = T.kvd[2 * myj] if with_mem else ks(myj)
        vsrc = T.kvd[2 * myj + 1] if with_mem else vs(myj)

        g.wait_ge(sem.ldq, 16)
        write([cores[other]], T.qoth[:, 0:W], T.qown[:, 0:W], sem.qa, chip_mask(rank))
        arrived(g, myj, "ka")
        write([cores[r] for r in served], ks(myj), ksrc, sem["ka%d" % myj], chip_mask(rank))
        arrived(g, myj, "va")
        write([cores[r] for r in served], vs(myj), vsrc, sem["va%d" % myj], chip_mask(rank))
        for n, job in enumerate(ja):
            g.wait_ge(sem["cp%d" % n], 1)
            write([cores[other]], T.land[:, job[3]:job[4]], T.obuf[:, job[3]:job[4]], sem["pa%d" % n],
                  chip_mask(rank))

        if with_mem:
            arrived(g.sync, myj, "ka")
            g.sync.dma_start(ks(myj), ksrc).then_inc(sem.ldk, 16)
            arrived(g.scalar, myj, "va")
            g.scalar.dma_start(vs(myj), vsrc).then_inc(sem.ldv, 16)
            te.wait_ge(sem.ldk, 16)
        else:
            arrived(te, myj, "ka")
        if ja:
            te.wait_ge(sem.qa, _count(chip_mask(other)))
            mm_s(ja)
        te.wait_ge(sem.ldq, 16)
        mm_s(jo)
        if with_mem:
            te.wait_ge(sem.ldv, 16)
        else:
            arrived(te, myj, "va")
        mm_o(ja)
        mm_o(jo)
        relu(ja)
        relu(jo)
        out(ja, T.obuf, "cp")
        out(jo, T.ybuf, "fin", T.land, _count(chip_mask(other)), 1 if with_mem else len(jo))

    hs = _halves(W)
    for n, (c0, c1) in enumerate(hs):
        qu = g.sync if n == len(hs) - 1 else g.scalar
        qu.wait_ge(sem["fin%d" % n], 1)
        qu.dma_start(T.y[:, c0:c1], T.ybuf[:, c0:c1]).then_inc(sem["st%d" % n], 16)
        qu.wait_ge(sem["st%d" % n], 16)
    if sent[0]:
        g.wait_ge(sem.snt, sent[0])
